import numpy as np
import ml_dtypes


def mxq(x, axis, fmt="e4m3"):
    dtype, down = {"e4m3": (ml_dtypes.float8_e4m3fn, 7), "e5m2": (ml_dtypes.float8_e5m2, 14)}[fmt]
    v = np.moveaxis(np.asarray(x, np.float32).astype(ml_dtypes.bfloat16).astype(np.float64), axis, -1)
    blocks = v.reshape(v.shape[:-1] + (-1, 32))
    amax = np.abs(blocks).max(-1, keepdims=True)
    byte = np.maximum(np.where(amax > 0, np.frexp(amax)[1] - 1 + 127, 0) - down, 1)
    scale = np.exp2(byte - 127.0)
    codes = (blocks / scale).astype(np.float32).astype(dtype).astype(np.float64)
    return np.moveaxis((codes * scale).reshape(v.shape), -1, axis)


WIDE = False


def mx_kscale(k):
    if not WIDE:
        return np.ones(k)
    levels = np.array([10, -10, 5, -5, 0])
    if k % 512:
        return np.exp2(np.random.permutation(np.resize(levels, k // 32))).repeat(32)
    a = np.empty((k // 512, 16))
    for p in range(k // 512):
        a[p, :8] = np.random.permutation(np.resize(levels, 8))
        for g in range(8):
            far = levels[np.abs(levels - a[p, g]) >= 10]
            a[p, g + 8] = far[np.random.randint(len(far))]
    return np.exp2(a.ravel()).repeat(32)


def f64(x):
    return np.asarray(x).astype(np.float64)


def striped(idx):
    return np.tile(idx.reshape(-1, 16).T, (8, 1)).astype(np.uint16)


def unstriped(offs):
    return offs[:16].T.reshape(-1).astype(np.int64)


E2M1 = np.array([0.0, 0.5, 1.0, 1.5, 2.0, 3.0, 4.0, 6.0, -0.0, -0.5, -1.0, -1.5, -2.0, -3.0, -4.0, -6.0])


def pack_weight(w, fmt):
    k, n = w.shape
    w = f64(np.asarray(w, np.float32).astype(ml_dtypes.bfloat16)).reshape(k // 32, 32, n)
    amax = np.abs(w).max(1)
    if fmt == "e4m3":
        byte = np.frexp(amax)[1] - 1 + 127 - 7
    else:
        mant, ex = np.frexp(amax / 6.0)
        byte = np.where(mant > 0.5, ex, ex - 1) + 127
    byte = np.clip(np.where(amax > 0, byte, 1), 1, 254)
    scaled = (w * np.exp2(127.0 - byte)[:, None, :]).reshape(k, n).astype(np.float32)
    by_word = np.ascontiguousarray(scaled.reshape(k // 512, 128, 4, n).transpose(0, 1, 3, 2))
    if fmt == "e4m3":
        words = by_word.astype(ml_dtypes.float8_e4m3fn).view(np.uint8)
    else:
        c = by_word.astype(ml_dtypes.float4_e2m1fn).view(np.uint8) & 0xF
        words = (c[..., 0::2] | (c[..., 1::2] << 4)).reshape(k // 512, 128, 2 * n)
    return np.ascontiguousarray(words), np.ascontiguousarray(byte.astype(np.uint8).reshape(k // 512, 16, n))


def unpack_weight(words, scales, fmt):
    g, _, n = scales.shape
    words = np.ascontiguousarray(words).reshape(g, 128, n, -1)
    if fmt == "e4m3":
        vals = words.view(ml_dtypes.float8_e4m3fn).astype(np.float64)
    else:
        nib = np.empty((g, 128, n, 4), np.uint8)
        nib[..., 0::2] = words & 0xF
        nib[..., 1::2] = words >> 4
        vals = E2M1[nib]
    vals = vals * np.repeat(np.exp2(scales.astype(np.float64) - 127.0), 8, axis=1)[..., None]
    return vals.transpose(0, 1, 3, 2).reshape(g * 512, n)


K, T, E, C, N = 512, 2560, 6, 256, 512


def by_expert(wq, xq):
    return np.concatenate([wq[e].T @ xq[:, e * C:(e + 1) * C] for e in range(E)], axis=1)


def setup_inputs():
    n = np.random.standard_normal
    s = mx_kscale(K)[:, None]
    w = [pack_weight(m, "e2m1") for m in n((E, K, N)) / np.sqrt(K) / s[None]]
    return {
        "xT": (n((K, T)) * s).astype(np.float32),
        "w_words": np.stack([m[0] for m in w]),
        "w_scales": np.stack([m[1] for m in w]),
        "gate": np.tile(np.random.uniform(0.2, 1.0, E * C), (N, 1)).astype(np.float32),
        "offs": striped(np.random.permutation(T)[:E * C]),
    }


def reference(xT, w_words, w_scales, gate, offs):
    idx = unstriped(offs)
    w = np.stack([unpack_weight(w_words[e], w_scales[e], "e2m1") for e in range(E)])
    xq = mxq(f64(xT)[:, idx], 0, "e4m3")
    y = by_expert(w, xq)
    out = np.zeros((N, T))
    out[:, idx] = f64(gate) * y
    return out

import concourse.mybir as mybir

K, T, E, C, N = 512, 2560, 6, 256, 512
P = 128
SLOTS = E * C
FLOPS = 2 * K * N * SLOTS

F32 = mybir.dt.float32
BF16 = mybir.dt.bfloat16
I32 = mybir.dt.int32
U32 = mybir.dt.uint32
U16 = mybir.dt.uint16
U8 = mybir.dt.uint8
FP8X4 = mybir.dt.float8_e4m3fn_x4
FP4X4 = mybir.dt.float4_e2m1fn_x4
MULT = mybir.AluOpType.mult

WIDTHS = (512, 512, 512, 512, 256, 256)
GROUP = 512
NT = N // P


def tile_moe_pln_lin_none_kernel(tc, xT, w_words, w_scales, gate, offs, out):
    nc = tc.nc
    with (
        tc.tile_pool(name="held", bufs=1) as held,
        tc.psum_pool(name="psum", bufs=8) as psum,
    ):
        offsets = held.tile([P, SLOTS // 16], U16, name="offsets")
        codes = held.tile([P, T], U32, name="codes", align_bytes=64)
        scales = held.tile([P, T], U8, name="scales", align_bytes=64)
        words = held.tile([P, E, 2 * N], U8, name="words", align_bytes=64)
        wplane = held.tile([P, E, N], U8, name="wplane", align_bytes=64)
        windows = [held.tile([P, T], F32, name=f"window{t}") for t in range(NT)]
        gates = [held.tile([P, SLOTS], F32, name=f"gate{t}") for t in range(NT)]
        results = [held.tile([P, SLOTS], F32, name=f"result{t}") for t in range(NT)]

        nc.gpsimd.memset(scales[:].bitcast(I32), 0)
        nc.gpsimd.memset(wplane[:].rearrange("p e n -> p (e n)").bitcast(I32), 0)

        x_rows = xT.rearrange("(p j) w -> p j w", j=4)
        raws, rounded = [], []
        first = 0
        for i, width in enumerate(WIDTHS):
            raw = held.tile([P, 4, width], F32, name=f"raw{i}")
            nc.sync.dma_start(raw[:], x_rows[:, :, first : first + width])
            raws.append(raw)
            rounded.append(held.tile([P, width, 4], BF16, name=f"rounded{i}", align_bytes=64))
            first += width
        nc.sync.dma_start(offsets[:], offs)
        nc.sync.dma_start(
            words[:].rearrange("p e b -> p (e b)").bitcast(I32).rearrange("p (e b) -> p e b", e=E),
            w_words.bitcast(I32).rearrange("e a p b -> p (e a) b"),
        )
        plane_words = wplane[:].rearrange("p e n -> p (e n)").bitcast(I32).rearrange("p (e n) -> p e n", e=E)
        scale_rows = w_scales.bitcast(I32).rearrange("e a q n -> q (e a) n")
        for quad in range(4):
            nc.sync.dma_start(plane_words[32 * quad : 32 * quad + 4], scale_rows[4 * quad : 4 * quad + 4])
        for t in range(NT):
            nc.sync.dma_start(gates[t][:], gate[P * t : P * (t + 1), :])

        for t in range(NT):
            nc.vector.memset(windows[t][:], 0.0)

        first = 0
        for i, width in enumerate(WIDTHS):
            cut = width * 5 // 8
            src = raws[i][:].rearrange("p j w -> p w j")
            nc.scalar.copy(rounded[i][:, cut:, :], src[:, cut:, :])
            nc.vector.tensor_copy(rounded[i][:, :cut, :], src[:, :cut, :])
            nc.vector.quantize_mx(
                out=codes[:, first : first + width].bitcast(FP8X4),
                scales=scales[:, first : first + width],
                in_=rounded[i][:].rearrange("p w j -> p (w j)"),
            )
            first += width

        for g in range(SLOTS // GROUP):
            slots = slice(g * GROUP, (g + 1) * GROUP)
            listed = offsets[:, g * GROUP // 16 : (g + 1) * GROUP // 16]
            slot_codes = held.tile([P, GROUP], U32, name=f"slot_codes{g}", align_bytes=64)
            slot_scales = held.tile([P, GROUP], U8, name=f"slot_scales{g}", align_bytes=64)
            nc.vector.tensor_copy(slot_codes[:], codes[:].indirect(listed))
            nc.vector.tensor_copy(slot_scales[:], scales[:].indirect(listed))
            for t in range(NT):
                bank = psum.tile([P, GROUP], F32, name="bank")
                for half in range(GROUP // C):
                    e = g * GROUP // C + half
                    cols = slice(half * C, (half + 1) * C)
                    nc.tensor.matmul_mx(
                        out=bank[:, cols],
                        lhsT=words[:, e, 2 * P * t : 2 * P * (t + 1)].bitcast(FP4X4),
                        lhsT_scale=wplane[:, e, P * t : P * (t + 1)],
                        rhs=slot_codes[:, cols].bitcast(FP8X4),
                        rhs_scale=slot_scales[:, cols],
                        start=True,
                        stop=True,
                    )
                nc.scalar.copy(results[t][:, slots], bank[:])

        for t in range(NT):
            pieces = [(g * GROUP, (g + 1) * GROUP) for g in range(SLOTS // GROUP)] if t == 0 else [(0, SLOTS)]
            for a, b in pieces:
                nc.vector.tensor_tensor(
                    windows[t][:].indirect(offsets[:, a // 16 : b // 16]),
                    results[t][:, a:b],
                    gates[t][:, a:b],
                    MULT,
                )
            half = T // 2
            nc.sync.dma_start(out[P * t : P * (t + 1), :half], windows[t][:, :half])
            nc.scalar.dma_start(out[P * t : P * (t + 1), half:], windows[t][:, half:])
